import numpy as np
import ml_dtypes


def mxq(x, axis, fmt="e4m3"):
    dtype, down = {"e4m3": (ml_dtypes.float8_e4m3fn, 7), "e5m2": (ml_dtypes.float8_e5m2, 14)}[fmt]
    v = np.moveaxis(np.asarray(x, np.float32).astype(ml_dtypes.bfloat16).astype(np.float64), axis, -1)
    blocks = v.reshape(v.shape[:-1] + (-1, 32))
    amax = np.abs(blocks).max(-1, keepdims=True)
    byte = np.maximum(np.where(amax > 0, np.frexp(amax)[1] - 1 + 127, 0) - down, 1)
    scale = np.exp2(byte - 127.0)
    codes = (blocks / scale).astype(np.float32).astype(dtype).astype(np.float64)
    return np.moveaxis((codes * scale).reshape(v.shape), -1, axis)


WIDE = False


def mx_kscale(k):
    if not WIDE:
        return np.ones(k)
    levels = np.array([18, -18])
    if k % 512:
        return np.exp2(np.random.permutation(np.resize(levels, k // 32))).repeat(32)
    a = np.empty((k // 512, 16))
    for p in range(k // 512):
        a[p, :8] = np.random.permutation(np.resize(levels, 8))
        for g in range(8):
            far = levels[np.abs(levels - a[p, g]) >= 10]
            a[p, g + 8] = far[np.random.randint(len(far))]
    return np.exp2(a.ravel()).repeat(32)


def f64(x):
    return np.asarray(x).astype(np.float64)


def striped(idx):
    return np.tile(np.asarray(idx).reshape(-1, 16).T, (8, 1)).astype(np.uint16)


def unstriped(offs):
    return offs[:16].T.reshape(-1).astype(np.int64)


E2M1 = np.array([0.0, 0.5, 1.0, 1.5, 2.0, 3.0, 4.0, 6.0, -0.0, -0.5, -1.0, -1.5, -2.0, -3.0, -4.0, -6.0])


def pack_weight(w, fmt):
    k, n = w.shape
    w = f64(np.asarray(w, np.float32).astype(ml_dtypes.bfloat16)).reshape(k // 32, 32, n)
    amax = np.abs(w).max(1)
    if fmt == "e4m3":
        byte = np.frexp(amax)[1] - 1 + 127 - 7
    else:
        mant, ex = np.frexp(amax / 6.0)
        byte = np.where(mant > 0.5, ex, ex - 1) + 127
    byte = np.clip(np.where(amax > 0, byte, 1), 1, 254)
    scaled = (w * np.exp2(127.0 - byte)[:, None, :]).reshape(k, n).astype(np.float32)
    by_word = np.ascontiguousarray(scaled.reshape(k // 512, 128, 4, n).transpose(0, 1, 3, 2))
    if fmt == "e4m3":
        words = by_word.astype(ml_dtypes.float8_e4m3fn).view(np.uint8)
    else:
        c = by_word.astype(ml_dtypes.float4_e2m1fn).view(np.uint8) & 0xF
        words = (c[..., 0::2] | (c[..., 1::2] << 4)).reshape(k // 512, 128, 2 * n)
    return np.ascontiguousarray(words), np.ascontiguousarray(byte.astype(np.uint8).reshape(k // 512, 16, n))


def unpack_weight(words, scales, fmt):
    g, _, n = scales.shape
    words = np.ascontiguousarray(words).reshape(g, 128, n, -1)
    if fmt == "e4m3":
        vals = words.view(ml_dtypes.float8_e4m3fn).astype(np.float64)
    else:
        nib = np.empty((g, 128, n, 4), np.uint8)
        nib[..., 0::2] = words & 0xF
        nib[..., 1::2] = words >> 4
        vals = E2M1[nib]
    vals = vals * np.repeat(np.exp2(scales.astype(np.float64) - 127.0), 8, axis=1)[..., None]
    return vals.transpose(0, 1, 3, 2).reshape(g * 512, n)


def planes(y):
    n, m = y.shape
    v = y.astype(np.float32).astype(ml_dtypes.bfloat16).astype(np.float64).reshape(n // 32, 32, m)
    top = np.abs(v).max(1)
    byte = np.clip(np.where(top > 0, np.frexp(top)[1] - 1 + 127 - 7, 1), 1, 254)
    codes = (v * np.exp2(127.0 - byte)[:, None, :]).reshape(n, m).astype(np.float32).astype(ml_dtypes.float8_e4m3fn).view(np.uint8)
    words = codes.reshape(n // 512, 128, 4, m).transpose(0, 1, 3, 2)
    return np.ascontiguousarray(words), np.ascontiguousarray(byte.astype(np.uint8).reshape(n // 512, 16, m))


V, K, E, D, DV = 512, 2, 1024, 512, 1024


def setup_inputs():
    n = np.random.standard_normal
    v = mx_kscale(DV)[:, None]
    coarse = lambda x: x.astype(np.float32).astype(ml_dtypes.bfloat16).astype(np.float64)
    wp = pack_weight(n((DV, D)) / np.sqrt(DV) / v, "e4m3")
    return {
        "dyT": (coarse(n((DV, V))) * v).astype(np.float32),
        "hE": coarse(n((DV, E))).astype(np.float32),
        "ew": np.tile(np.random.randint(8, 33, E) / 16.0, (128, 1)).astype(np.float32),
        "w_words": wp[0],
        "w_scales": wp[1],
        "offs": striped(np.random.randint(0, V, E)),
        "offs2": striped(np.random.permutation(E)),
    }


def reference(dyT, hE, ew, w_words, w_scales, offs, offs2):
    h = f64(hE)
    dz = f64(ew)[:1] * f64(dyT)[:, unstriped(offs)] * 2.0 * np.maximum(h, 0.0)
    dm = unpack_weight(w_words, w_scales, "e4m3").T @ mxq(dz, 0, "e5m2")
    out_0 = dm[:, unstriped(offs2)].reshape(D, V, K).sum(-1)
    return (out_0,) + planes(out_0)

@@ -1,0 +1,230 @@
+from contextlib import ExitStack
+
+import concourse.mybir as mybir
+from concourse.masks import make_identity
+
+V, K, E, D, DV = 512, 2, 1024, 512, 1024
+FLOPS = 2 * DV * D * E
+BYTES = 4 * DV * V + 4 * DV * E + 4 * E + DV * D + DV * D // 32 + 2 * 2 * 128 * 64 + 4 * D * V + D * V + D * V // 32
+
+F32 = mybir.dt.float32
+BF16 = mybir.dt.bfloat16
+I32 = mybir.dt.int32
+U16 = mybir.dt.uint16
+U8 = mybir.dt.uint8
+E4 = mybir.dt.float8_e4m3fn_x4
+E5 = mybir.dt.float8_e5m2_x4
+MULT = mybir.AluOpType.mult
+ADD = mybir.AluOpType.add
+RELU = mybir.ActivationFunctionType.Relu
+COPY = mybir.ActivationFunctionType.Copy
+
+P = 128
+LANES = 4
+PASSES = DV // (P * LANES)
+HALF = 512
+HALVES = E // HALF
+CHUNK = 256
+SPARE = 32
+NODE_PIECES = ((0, 256), (256, 384), (384, 512))
+
+
+def tile_attend_gmp_pl_ew_kernel(tc, dyT, hE, ew, w_words, w_scales, offs, offs2, out_0, out_1, out_2):
+    nc = tc.nc
+    with ExitStack() as ctx:
+        keep = ctx.enter_context(tc.tile_pool(name="keep", bufs=1))
+        ring = ctx.enter_context(tc.tile_pool(name="ring", bufs=3))
+        psum = ctx.enter_context(tc.psum_pool(name="psum", bufs=1))
+
+        dy_rows = dyT.rearrange("(o p t) v -> o t p v", p=P, t=LANES)
+        h_rows = hE.rearrange("(o p t) e -> o p t e", p=P, t=LANES)
+        units = [(half, o) for half in range(HALVES) for o in range(PASSES)]
+
+        dst = keep.tile([P, E // 16], U16, name="dst")
+        src = keep.tile([P, E // 16], U16, name="src")
+        nc.sync.dma_start(dst[:], offs)
+
+        warm = keep.tile([P, 1], F32, name="warm")
+        warm2 = keep.tile([P, 1], F32, name="warm2")
+        nc.vector.memset(warm[:], 0.0)
+        nc.scalar.activation(warm2[:], warm[:], RELU, scale=2.0)
+
+        ident = keep.tile([P, P], F32, name="ident")
+        make_identity(nc, ident[:])
+
+        dy = {}
+        for o in range(PASSES):
+            for t in range(LANES):
+                dy[o, t] = keep.tile([P, V + SPARE], F32, name="dy%d%d" % (o, t))
+                nc.vector.memset(dy[o, t][:, V:], 0.0)
+        ws_raw = keep.tile([P, PASSES, D], U8, name="ws_raw")
+        nc.vector.memset(ws_raw[:].bitcast(I32), 0)
+
+        h = {}
+        for half, o in units:
+            h[half, o] = keep.tile([P, LANES, HALF], F32, name="h%d%d" % (half, o))
+        ew_sq = keep.tile([P, P], F32, name="ew_sq")
+        ew_row = keep.tile([P, CHUNK], F32, name="ew_row")
+        w_raw = keep.tile([P, PASSES, D], I32, name="w_raw")
+
+        for o in range(PASSES):
+            for t in range(LANES):
+                nc.sync.dma_start(dy[o, t][:, :V], dy_rows[o, t])
+                nc.sync.dma_start(h[0, o][:, t, :], h_rows[o, :, t, :HALF])
+            if o == 0:
+                nc.sync.dma_start(ew_sq[:], ew[: P * P // E, :].rearrange("r (b e) -> (r b) e", e=P))
+        for q in range(4):
+            nc.sync.dma_start(
+                ws_raw[32 * q : 32 * q + 4, :, :].bitcast(I32),
+                w_scales[:, 4 * q : 4 * q + 4, :].rearrange("o f d -> f o d").bitcast(I32),
+            )
+        nc.sync.dma_start(h[1, 0][:], h_rows[0, :, :, HALF:])
+        nc.sync.dma_start(w_raw[:], w_words.rearrange("o p d r -> p o (d r)").bitcast(I32))
+        nc.sync.dma_start(h[1, 1][:], h_rows[1, :, :, HALF:])
+        nc.sync.dma_start(ew_row[:], ew[:, E - CHUNK :])
+        nc.sync.dma_start(src[:], offs2)
+
+        ew_ps = psum.tile([P, LANES, P], F32, name="ew_ps", tag="turned", bufs=3)
+        nc.tensor.transpose(ew_ps[:, 0, :], ew_sq[:], ident[:])
+        ew_col = keep.tile([P, E // P], F32, name="ew_col")
+
+        codes, scales, r, u = {}, {}, {}, {}
+        for half, o in units:
+            codes[half, o] = keep.tile([P, HALF], I32, name="codes%d%d" % (half, o), align_bytes=64)
+            scales[half, o] = keep.tile([P, HALF], U8, name="scales%d%d" % (half, o), align_bytes=64)
+            r[half, o] = keep.tile([P, LANES, HALF], F32, name="r%d%d" % (half, o))
+            u[half, o] = keep.tile([P, LANES, HALF], F32, name="u%d%d" % (half, o))
+
+        def relu(unit):
+            for t in range(LANES):
+                nc.scalar.activation(r[unit][:, t, :], h[unit][:, t, :], RELU, scale=2.0)
+
+        def look_up(unit, e0, e1):
+            half, o = unit
+            picks = dst[:, (half * HALF + e0) // 16 : (half * HALF + e1) // 16]
+            for t in range(LANES):
+                nc.vector.tensor_tensor(u[unit][:, t, e0:e1], dy[o, t][:].indirect(picks), r[unit][:, t, e0:e1], MULT)
+
+        def quantise(unit, e0, grouped):
+            nc.vector.quantize_mx(
+                out=codes[unit][:, e0 : e0 + CHUNK].bitcast(E5),
+                scales=scales[unit][:, e0 : e0 + CHUNK],
+                in_=grouped[:],
+            )
+
+        def weigh_turned(unit, e0):
+            half, o = unit
+            back = psum.tile([P, CHUNK // P, 2, P], F32, name="back", tag="back", bufs=2)
+            for b in range(CHUNK // P):
+                c0 = e0 + b * P
+                turned = psum.tile([P, LANES, P], F32, name="turned", tag="turned", bufs=3)
+                for t in range(LANES):
+                    nc.tensor.transpose(turned[:, t, :], u[unit][:, t, c0 : c0 + P], ident[:])
+                pairs = ring.tile([P, 2 * P * 2], BF16, name="pairs")
+                block = (half * HALF + c0) // P
+                nc.scalar.activation(
+                    pairs[:].rearrange("e (w p s) -> e w p s", w=2, s=2),
+                    turned[:].rearrange("e (w s) p -> e w p s", s=2),
+                    COPY,
+                    scale=ew_col[:, block : block + 1],
+                )
+                for w in range(2):
+                    nc.tensor.transpose(back[:, b, w, :], pairs[:].bitcast(F32)[:, w * P : (w + 1) * P], ident[:])
+            grouped = ring.tile([P, CHUNK * LANES], BF16, name="grouped", align_bytes=64)
+            nc.scalar.copy(
+                grouped[:].bitcast(F32).rearrange("p (b e w) -> p b e w", w=2, e=P),
+                back[:].rearrange("p b w e -> p b e w"),
+            )
+            quantise(unit, e0, grouped)
+
+        def weigh_direct(unit, e0):
+            grouped = ring.tile([P, CHUNK * LANES], BF16, name="grouped", align_bytes=64)
+            nc.vector.tensor_tensor(
+                grouped[:].rearrange("p (c i t) -> p c t i", i=4, t=LANES),
+                u[unit][:, :, e0 : e0 + CHUNK].rearrange("p t (c i) -> p c t i", i=4),
+                ew_row[:].rearrange("p (c i) -> p c i", i=4).unsqueeze(2).to_broadcast([P, CHUNK // 4, LANES, 4]),
+                MULT,
+            )
+            quantise(unit, e0, grouped)
+
+        w_dealt = keep.tile([P, PASSES, D], I32, name="w_dealt", align_bytes=64)
+        ws_dealt = keep.tile([P, PASSES, D], U8, name="ws_dealt", align_bytes=64)
+
+        def deal():
+            for o in range(PASSES):
+                nc.vector.tensor_copy(
+                    w_dealt[:, o, :].rearrange("p (t c i) -> p c t i", t=LANES, i=4),
+                    w_raw[:, o, :].rearrange("p (c i t) -> p c t i", t=LANES, i=4),
+                )
+            nc.vector.tensor_copy(
+                ws_dealt[:].rearrange("p o (t m) -> p o t m", t=LANES),
+                ws_raw[:].rearrange("p o (m t) -> p o t m", t=LANES),
+            )
+
+        dm = [keep.tile([P, E], F32, name="dm%d" % t) for t in range(LANES)]
+
+        def multiply(half, t):
+            acc = psum.tile([P, HALF], F32, name="acc", tag="acc", bufs=3)
+            for o in range(PASSES):
+                nc.tensor.matmul_mx(
+                    out=acc[:],
+                    lhsT=w_dealt[:, o, t * P : (t + 1) * P].bitcast(E4),
+                    lhsT_scale=ws_dealt[:, o, t * P : (t + 1) * P],
+                    rhs=codes[half, o][:].bitcast(E5),
+                    rhs_scale=scales[half, o][:],
+                    start=(o == 0),
+                    stop=(o == PASSES - 1),
+                )
+            nc.scalar.copy(dm[t][:, half * HALF : (half + 1) * HALF], acc[:])
+
+        relu(units[0])
+        nc.scalar.copy(ew_col[:], ew_ps[:, 0, : E // P])
+        look_up(units[0], 0, HALF)
+        for n in range(1, len(units)):
+            relu(units[n])
+            if n < len(units) - 1:
+                look_up(units[n], 0, HALF)
+            else:
+                look_up(units[n], 0, CHUNK)
+            for e0 in range(0, HALF, CHUNK):
+                weigh_turned(units[n - 1], e0)
+            if n == 2:
+                deal()
+        last = units[-1]
+        look_up(last, CHUNK, HALF)
+        weigh_turned(last, 0)
+        weigh_direct(last, CHUNK)
+        for half in range(HALVES):
+            for t in range(LANES):
+                multiply(half, t)
+
+        y_rows = out_0.rearrange("(p t) x -> p t x", t=LANES)
+        y_words = out_1[0].rearrange("p x r -> p (x r)").bitcast(I32)
+        y_codes = keep.tile([P, V], I32, name="y_codes", align_bytes=64)
+        y_scales = keep.tile([P, V], U8, name="y_scales", align_bytes=64)
+        for x0, x1 in NODE_PIECES:
+            n = x1 - x0
+            picked = keep.tile([P, LANES, n, K], F32, name="picked%d" % x0)
+            for t in range(LANES):
+                nc.vector.tensor_copy(
+                    picked[:, t].rearrange("p x j -> p (x j)"),
+                    dm[t][:].indirect(src[:, K * x0 // 16 : K * x1 // 16]),
+                )
+            y = keep.tile([P, LANES, n], F32, name="y%d" % x0)
+            nc.vector.tensor_tensor(y[:], picked[:, :, :, 0], picked[:, :, :, 1], ADD)
+            nc.sync.dma_start(y_rows[:, :, x0:x1], y[:])
+            y_grouped = keep.tile([P, n * LANES], BF16, name="y_grouped%d" % x0, align_bytes=64)
+            if x1 < V:
+                nc.scalar.activation(
+                    y_grouped[:].rearrange("p (x t) -> p x t", t=LANES), y[:].rearrange("p t x -> p x t"), COPY
+                )
+            else:
+                nc.vector.tensor_copy(
+                    y_grouped[:].rearrange("p (c i t) -> p c t i", i=4, t=LANES),
+                    y[:].rearrange("p t (c i) -> p c t i", i=4),
+                )
+            nc.vector.quantize_mx(out=y_codes[:, x0:x1].bitcast(E4), scales=y_scales[:, x0:x1], in_=y_grouped[:])
+            nc.scalar.dma_start(y_words[:, x0:x1], y_codes[:, x0:x1])
+        for q in range(4):
+            queue = nc.sync if q % 2 == 0 else nc.scalar
+            queue.dma_start(out_2[0, 4 * q : 4 * q + 4, :].bitcast(I32), y_scales[32 * q : 32 * q + 4, :].bitcast(I32))

@@ -26,23 +26,22 @@ HALF = 512
 HALVES = E // HALF
 CHUNK = 256
 SPARE = 32
-NODE_PIECES = ((0, 256), (256, 384), (384, 512))
+TURNED_NODES = 256
 
 
 def tile_attend_gmp_pl_ew_kernel(tc, dyT, hE, ew, w_words, w_scales, offs, offs2, out_0, out_1, out_2):
     nc = tc.nc
     with ExitStack() as ctx:
         keep = ctx.enter_context(tc.tile_pool(name="keep", bufs=1))
-        ring = ctx.enter_context(tc.tile_pool(name="ring", bufs=3))
+        ring = ctx.enter_context(tc.tile_pool(name="ring", bufs=8))
         psum = ctx.enter_context(tc.psum_pool(name="psum", bufs=1))
 
         dy_rows = dyT.rearrange("(o p t) v -> o t p v", p=P, t=LANES)
         h_rows = hE.rearrange("(o p t) e -> o p t e", p=P, t=LANES)
-        units = [(half, o) for half in range(HALVES) for o in range(PASSES)]
+        units = [(half, o) for o in range(PASSES) for half in range(HALVES)]
 
         dst = keep.tile([P, E // 16], U16, name="dst")
         src = keep.tile([P, E // 16], U16, name="src")
-        nc.sync.dma_start(dst[:], offs)
 
         warm = keep.tile([P, 1], F32, name="warm")
         warm2 = keep.tile([P, 1], F32, name="warm2")
@@ -62,169 +61,269 @@ def tile_attend_gmp_pl_ew_kernel(tc, dyT, hE, ew, w_words, w_scales, offs, offs2
 
         h = {}
         for half, o in units:
-            h[half, o] = keep.tile([P, LANES, HALF], F32, name="h%d%d" % (half, o))
+            for t in range(LANES):
+                h[half, o, t] = keep.tile([P, HALF], F32, name="h%d%d%d" % (half, o, t), tag="h%d%d%d" % (half, o, t), align_bytes=64)
         ew_sq = keep.tile([P, P], F32, name="ew_sq")
         ew_row = keep.tile([P, CHUNK], F32, name="ew_row")
-        w_raw = keep.tile([P, PASSES, D], I32, name="w_raw")
+        w_raw = keep.tile([P, PASSES, D], I32, name="w_raw", tag="w_raw", align_bytes=64)
 
-        for o in range(PASSES):
+        def load_h(unit, t, e0, e1):
+            half, o = unit
+            nc.sync.dma_start(h[half, o, t][:, e0:e1], h_rows[o, :, t, half * HALF + e0 : half * HALF + e1])
+
+        for t in range(LANES):
+            load_h(units[0], t, 0, CHUNK)
+            if t == 0:
+                nc.sync.dma_start(dst[:], offs)
+            nc.sync.dma_start(dy[0, t][:, :V], dy_rows[0, t])
+        nc.sync.dma_start(ew_sq[:], ew[: P * P // E, :].rearrange("r (b e) -> (r b) e", e=P))
+        for t in range(LANES):
+            load_h(units[0], t, CHUNK, HALF)
+        for unit in units[1:3]:
             for t in range(LANES):
-                nc.sync.dma_start(dy[o, t][:, :V], dy_rows[o, t])
-                nc.sync.dma_start(h[0, o][:, t, :], h_rows[o, :, t, :HALF])
-            if o == 0:
-                nc.sync.dma_start(ew_sq[:], ew[: P * P // E, :].rearrange("r (b e) -> (r b) e", e=P))
+                load_h(unit, t, 0, HALF)
+        for t in range(LANES):
+            nc.sync.dma_start(dy[1, t][:, :V], dy_rows[1, t])
+        for t in range(LANES):
+            load_h(units[3], t, 0, HALF)
         for q in range(4):
             nc.sync.dma_start(
                 ws_raw[32 * q : 32 * q + 4, :, :].bitcast(I32),
                 w_scales[:, 4 * q : 4 * q + 4, :].rearrange("o f d -> f o d").bitcast(I32),
             )
-        nc.sync.dma_start(h[1, 0][:], h_rows[0, :, :, HALF:])
         nc.sync.dma_start(w_raw[:], w_words.rearrange("o p d r -> p o (d r)").bitcast(I32))
-        nc.sync.dma_start(h[1, 1][:], h_rows[1, :, :, HALF:])
         nc.sync.dma_start(ew_row[:], ew[:, E - CHUNK :])
         nc.sync.dma_start(src[:], offs2)
 
-        ew_ps = psum.tile([P, LANES, P], F32, name="ew_ps", tag="turned", bufs=3)
+        ew_ps = psum.tile([P, LANES, P], F32, name="ew_ps", tag="h")
         nc.tensor.transpose(ew_ps[:, 0, :], ew_sq[:], ident[:])
         ew_col = keep.tile([P, E // P], F32, name="ew_col")
 
         codes, scales, r, u = {}, {}, {}, {}
         for half, o in units:
-            codes[half, o] = keep.tile([P, HALF], I32, name="codes%d%d" % (half, o), align_bytes=64)
             scales[half, o] = keep.tile([P, HALF], U8, name="scales%d%d" % (half, o), align_bytes=64)
-            r[half, o] = keep.tile([P, LANES, HALF], F32, name="r%d%d" % (half, o))
-            u[half, o] = keep.tile([P, LANES, HALF], F32, name="u%d%d" % (half, o))
 
-        def relu(unit):
-            for t in range(LANES):
-                nc.scalar.activation(r[unit][:, t, :], h[unit][:, t, :], RELU, scale=2.0)
+        def relu(unit, e0, e1, lanes=range(LANES), tag=None):
+            if (unit, e0) not in r:
+                name = "r%d%d%d" % (unit + (e0,))
+                r[unit, e0] = keep.tile([P, LANES, e1 - e0], F32, name=name, tag=tag or name, align_bytes=64)
+            for t in lanes:
+                nc.scalar.activation(r[unit, e0][:, t, :], h[unit + (t,)][:, e0:e1], RELU, scale=2.0)
 
-        def look_up(unit, e0, e1):
+        def look_up(unit, e0, e1, tag=None):
             half, o = unit
+            name = "u%d%d%d" % (half, o, e0)
+            u[unit, e0] = keep.tile([P, LANES, e1 - e0], F32, name=name, tag=tag or name, align_bytes=64)
             picks = dst[:, (half * HALF + e0) // 16 : (half * HALF + e1) // 16]
             for t in range(LANES):
-                nc.vector.tensor_tensor(u[unit][:, t, e0:e1], dy[o, t][:].indirect(picks), r[unit][:, t, e0:e1], MULT)
+                nc.vector.tensor_tensor(u[unit, e0][:, t, :], dy[o, t][:].indirect(picks), r[unit, e0][:, t, :], MULT)
 
-        def quantise(unit, e0, grouped):
+        def quantise(unit, e0, n, grouped):
+            if unit not in codes:
+                name = "codes%d%d" % unit
+                codes[unit] = keep.tile([P, HALF], I32, name=name, tag=name, align_bytes=64)
             nc.vector.quantize_mx(
-                out=codes[unit][:, e0 : e0 + CHUNK].bitcast(E5),
-                scales=scales[unit][:, e0 : e0 + CHUNK],
+                out=codes[unit][:, e0 : e0 + n].bitcast(E5),
+                scales=scales[unit][:, e0 : e0 + n],
                 in_=grouped[:],
             )
 
-        def weigh_turned(unit, e0):
+        back, grouped = {}, {}
+
+        def weigh(unit, e0, b, bank, back_bank, spent=None):
             half, o = unit
-            back = psum.tile([P, CHUNK // P, 2, P], F32, name="back", tag="back", bufs=2)
-            for b in range(CHUNK // P):
-                c0 = e0 + b * P
-                turned = psum.tile([P, LANES, P], F32, name="turned", tag="turned", bufs=3)
-                for t in range(LANES):
-                    nc.tensor.transpose(turned[:, t, :], u[unit][:, t, c0 : c0 + P], ident[:])
+            turned = psum.tile([P, LANES, P], F32, name="turned", tag=bank)
+            for t in range(LANES):
+                nc.tensor.transpose(turned[:, t, :], u[unit, e0][:, t, b * P : (b + 1) * P], ident[:])
+            if spent:
+                pairs = keep.tile([P, 2 * P * 2], BF16, name="pairs", tag="h%d%d%d" % spent, align_bytes=64)
+            else:
                 pairs = ring.tile([P, 2 * P * 2], BF16, name="pairs")
-                block = (half * HALF + c0) // P
-                nc.scalar.activation(
-                    pairs[:].rearrange("e (w p s) -> e w p s", w=2, s=2),
-                    turned[:].rearrange("e (w s) p -> e w p s", s=2),
-                    COPY,
-                    scale=ew_col[:, block : block + 1],
-                )
-                for w in range(2):
-                    nc.tensor.transpose(back[:, b, w, :], pairs[:].bitcast(F32)[:, w * P : (w + 1) * P], ident[:])
-            grouped = ring.tile([P, CHUNK * LANES], BF16, name="grouped", align_bytes=64)
-            nc.scalar.copy(
-                grouped[:].bitcast(F32).rearrange("p (b e w) -> p b e w", w=2, e=P),
-                back[:].rearrange("p b w e -> p b e w"),
+            block = (half * HALF + e0) // P + b
+            nc.scalar.activation(
+                pairs[:].rearrange("e (w p s) -> e w p s", w=2, s=2),
+                turned[:].rearrange("e (w s) p -> e w p s", s=2),
+                COPY,
+                scale=ew_col[:, block : block + 1],
             )
-            quantise(unit, e0, grouped)
+            back[unit, e0, b] = psum.tile([P, 2, P], F32, name="back", tag=back_bank)
+            for w in range(2):
+                nc.tensor.transpose(back[unit, e0, b][:, w, :], pairs[:].bitcast(F32)[:, w * P : (w + 1) * P], ident[:])
+
+        def regroup(unit, e0, b, tag=None, group=2):
+            if tag:
+                grouped[unit] = keep.tile([P, group * P * LANES], BF16, name="grouped", tag=tag, align_bytes=64)
+            elif b % group == 0:
+                grouped[unit] = ring.tile([P, group * P * LANES], BF16, name="grouped", align_bytes=64)
+            at = (b % group) * 2 * P
+            nc.scalar.copy(
+                grouped[unit][:].bitcast(F32)[:, at : at + 2 * P].rearrange("p (e w) -> p e w", w=2),
+                back[unit, e0, b][:].rearrange("p w e -> p e w"),
+            )
+            if b % group == group - 1:
+                quantise(unit, e0 + (b + 1 - group) * P, group * P, grouped[unit])
 
         def weigh_direct(unit, e0):
-            grouped = ring.tile([P, CHUNK * LANES], BF16, name="grouped", align_bytes=64)
+            grouped = keep.tile([P, CHUNK * LANES], BF16, name="grouped_last", align_bytes=64)
             nc.vector.tensor_tensor(
-                grouped[:].rearrange("p (c i t) -> p c t i", i=4, t=LANES),
-                u[unit][:, :, e0 : e0 + CHUNK].rearrange("p t (c i) -> p c t i", i=4),
-                ew_row[:].rearrange("p (c i) -> p c i", i=4).unsqueeze(2).to_broadcast([P, CHUNK // 4, LANES, 4]),
+                grouped[:].rearrange("p (c i t) -> p c t i", i=2, t=LANES),
+                u[unit, e0][:].rearrange("p t (c i) -> p c t i", i=2),
+                ew_row[:].rearrange("p (c i) -> p c i", i=2).unsqueeze(2).to_broadcast([P, CHUNK // 2, LANES, 2]),
                 MULT,
             )
-            quantise(unit, e0, grouped)
+            quantise(unit, e0, CHUNK, grouped)
 
-        w_dealt = keep.tile([P, PASSES, D], I32, name="w_dealt", align_bytes=64)
-        ws_dealt = keep.tile([P, PASSES, D], U8, name="ws_dealt", align_bytes=64)
+        w_dealt, ws_dealt = {}, {}
 
-        def deal():
-            for o in range(PASSES):
-                nc.vector.tensor_copy(
-                    w_dealt[:, o, :].rearrange("p (t c i) -> p c t i", t=LANES, i=4),
-                    w_raw[:, o, :].rearrange("p (c i t) -> p c t i", t=LANES, i=4),
-                )
+        def deal(pair, words_tag, scales_tag):
+            w_dealt[pair] = keep.tile([P, PASSES, 2, P], I32, name="w_dealt%d" % pair, tag=words_tag, align_bytes=64)
+            ws_dealt[pair] = keep.tile([P, PASSES, 2, P], U8, name="ws_dealt%d" % pair, tag=scales_tag, align_bytes=64)
+            lanes = slice(2 * pair, 2 * pair + 2)
             nc.vector.tensor_copy(
-                ws_dealt[:].rearrange("p o (t m) -> p o t m", t=LANES),
-                ws_raw[:].rearrange("p o (m t) -> p o t m", t=LANES),
+                w_dealt[pair][:].rearrange("p o s (c i) -> p o c s i", i=4),
+                w_raw[:].rearrange("p o (c i t) -> p o c t i", t=LANES, i=4)[:, :, :, lanes, :],
+            )
+            nc.vector.tensor_copy(
+                ws_dealt[pair][:],
+                ws_raw[:].rearrange("p o (m t) -> p o t m", t=LANES)[:, :, lanes, :],
             )
 
-        dm = [keep.tile([P, E], F32, name="dm%d" % t) for t in range(LANES)]
+        dm = {}
 
         def multiply(half, t):
-            acc = psum.tile([P, HALF], F32, name="acc", tag="acc", bufs=3)
+            acc = psum.tile([P, HALF], F32, name="acc", tag=late[(2 * t + half) % len(late)])
             for o in range(PASSES):
                 nc.tensor.matmul_mx(
                     out=acc[:],
-                    lhsT=w_dealt[:, o, t * P : (t + 1) * P].bitcast(E4),
-                    lhsT_scale=ws_dealt[:, o, t * P : (t + 1) * P],
+                    lhsT=w_dealt[t // 2][:, o, t % 2, :].bitcast(E4),
+                    lhsT_scale=ws_dealt[t // 2][:, o, t % 2, :],
                     rhs=codes[half, o][:].bitcast(E5),
                     rhs_scale=scales[half, o][:],
                     start=(o == 0),
                     stop=(o == PASSES - 1),
                 )
+            if t not in dm:
+                dm[t] = keep.tile([P, E], F32, name="dm%d" % t, tag="dm%d" % t)
             nc.scalar.copy(dm[t][:, half * HALF : (half + 1) * HALF], acc[:])
 
-        relu(units[0])
+        u0, u1, u2, u3 = units
+        relu(u0, 0, CHUNK)
         nc.scalar.copy(ew_col[:], ew_ps[:, 0, : E // P])
-        look_up(units[0], 0, HALF)
-        for n in range(1, len(units)):
-            relu(units[n])
-            if n < len(units) - 1:
-                look_up(units[n], 0, HALF)
-            else:
-                look_up(units[n], 0, CHUNK)
-            for e0 in range(0, HALF, CHUNK):
-                weigh_turned(units[n - 1], e0)
-            if n == 2:
-                deal()
-        last = units[-1]
-        look_up(last, CHUNK, HALF)
-        weigh_turned(last, 0)
-        weigh_direct(last, CHUNK)
-        for half in range(HALVES):
-            for t in range(LANES):
+        look_up(u0, 0, CHUNK)
+        relu(u0, CHUNK, HALF)
+        look_up(u0, CHUNK, HALF)
+        weigh(u0, 0, 0, "a", "a", u0 + (2,))
+        relu(u1, 0, HALF, range(1))
+        weigh(u0, 0, 1, "b", "c", u0 + (3,))
+        regroup(u0, 0, 0)
+        regroup(u0, 0, 1)
+        relu(u1, 0, HALF, range(1, LANES))
+        look_up(u1, 0, HALF)
+        weigh(u0, CHUNK, 0, "b", "b", u1 + (2,))
+        weigh(u0, CHUNK, 1, "a", "c", u1 + (3,))
+        regroup(u0, CHUNK, 0)
+        regroup(u0, CHUNK, 1)
+        relu(u2, 0, HALF)
+        look_up(u2, 0, HALF)
+        weigh(u1, 0, 0, "a", "a", u2 + (2,))
+        weigh(u1, 0, 1, "b", "b", u2 + (3,))
+        weigh(u1, 0, 2, "c", "c")
+        regroup(u1, 0, 0)
+        relu(u3, 0, CHUNK, range(2))
+        weigh(u1, 0, 3, "a", "d")
+        relu(u3, 0, CHUNK, range(2, LANES))
+        for b in range(1, 4):
+            regroup(u1, 0, b)
+        look_up(u3, 0, CHUNK)
+        weigh(u2, 0, 0, "a", "e")
+        weigh(u2, 0, 1, "b", "f")
+        relu(u3, CHUNK, HALF, range(0, 1), "u100")
+        weigh(u2, 0, 2, "c", "c")
+        relu(u3, CHUNK, HALF, range(1, 2))
+        weigh(u2, 0, 3, "d", "d")
+        relu(u3, CHUNK, HALF, range(2, 3))
+        regroup(u2, 0, 0)
+        relu(u3, CHUNK, HALF, range(3, 4))
+        look_up(u3, CHUNK, HALF)
+        weigh(u3, 0, 0, "a", "a")
+        regroup(u2, 0, 1)
+        weigh(u3, 0, 1, "b", "g")
+        regroup(u2, 0, 2)
+        regroup(u2, 0, 3)
+        weigh_direct(u3, CHUNK)
+        deal(0, "h112", "h113")
+        regroup(u3, 0, 0, "next_to_last", 1)
+        regroup(u3, 0, 1, "last", 1)
+        deal(1, "last", "w_raw")
+        late = ["b", "f", "b", "c", "a", "g", "d", "e"]
+        for t in range(LANES):
+            for half in range(HALVES):
                 multiply(half, t)
 
         y_rows = out_0.rearrange("(p t) x -> p t x", t=LANES)
         y_words = out_1[0].rearrange("p x r -> p (x r)").bitcast(I32)
         y_codes = keep.tile([P, V], I32, name="y_codes", align_bytes=64)
         y_scales = keep.tile([P, V], U8, name="y_scales", align_bytes=64)
-        for x0, x1 in NODE_PIECES:
-            n = x1 - x0
-            picked = keep.tile([P, LANES, n, K], F32, name="picked%d" % x0)
+
+        first = [keep.tile([P, K * TURNED_NODES], F32, name="first%d" % t, tag="first%d" % t, align_bytes=64) for t in range(LANES)]
+        for t in range(LANES):
+            nc.vector.tensor_copy(first[t][:], dm[t][:].indirect(src[:, : K * TURNED_NODES // 16]))
+        rows = {}
+        summed = [psum.tile([P, LANES, P], F32, name="summed", tag="bf"[b]) for b in range(TURNED_NODES // P)]
+        for t in range(LANES):
+            for b in range(TURNED_NODES // P):
+                for j in range(K):
+                    nc.tensor.matmul(
+                        summed[b][:, t, :], first[t][:, b * K * P + j : (b + 1) * K * P : K], ident[:],
+                        start=(j == 0), stop=(j == K - 1), is_transpose=True,
+                    )
+        for b in range(TURNED_NODES // P):
+            whole = keep.tile([P, LANES, P], F32, name="whole", tag="whole%d" % b, align_bytes=64)
+            nc.scalar.copy(whole[:], summed[b][:])
+            rows[b] = psum.tile([P, LANES, P], F32, name="rows", tag="ca"[b])
+            for t in range(LANES):
+                nc.tensor.transpose(rows[b][:, t, :], whole[:, t, :], ident[:])
+
+        def summed_on_vector(x0, tag):
+            picked = keep.tile([P, LANES * K * P], F32, name="picked", tag=tag, align_bytes=64)
+            y = keep.tile([P, LANES, P], F32, name="y%d" % x0)
             for t in range(LANES):
                 nc.vector.tensor_copy(
-                    picked[:, t].rearrange("p x j -> p (x j)"),
-                    dm[t][:].indirect(src[:, K * x0 // 16 : K * x1 // 16]),
+                    picked[:, t * K * P : (t + 1) * K * P],
+                    dm[t][:].indirect(src[:, K * x0 // 16 : K * (x0 + P) // 16]),
                 )
-            y = keep.tile([P, LANES, n], F32, name="y%d" % x0)
-            nc.vector.tensor_tensor(y[:], picked[:, :, :, 0], picked[:, :, :, 1], ADD)
-            nc.sync.dma_start(y_rows[:, :, x0:x1], y[:])
-            y_grouped = keep.tile([P, n * LANES], BF16, name="y_grouped%d" % x0, align_bytes=64)
-            if x1 < V:
-                nc.scalar.activation(
-                    y_grouped[:].rearrange("p (x t) -> p x t", t=LANES), y[:].rearrange("p t x -> p x t"), COPY
+            for pair in range(2):
+                nc.vector.tensor_tensor(
+                    y[:, 2 * pair : 2 * pair + 2, :].rearrange("p s x -> p (s x)"),
+                    picked[:, 2 * pair * K * P : 2 * (pair + 1) * K * P : K],
+                    picked[:, 2 * pair * K * P + 1 : 2 * (pair + 1) * K * P : K],
+                    ADD,
                 )
-            else:
-                nc.vector.tensor_copy(
-                    y_grouped[:].rearrange("p (c i t) -> p c t i", i=4, t=LANES),
-                    y[:].rearrange("p t (c i) -> p c t i", i=4),
-                )
-            nc.vector.quantize_mx(out=y_codes[:, x0:x1].bitcast(E4), scales=y_scales[:, x0:x1], in_=y_grouped[:])
-            nc.scalar.dma_start(y_words[:, x0:x1], y_codes[:, x0:x1])
+            nc.sync.dma_start(y_rows[:, :, x0 : x0 + P], y[:])
+            return y
+
+        def round_on_scalar(grouped, planes):
+            nc.scalar.activation(grouped.rearrange("p (x t) -> p x t", t=LANES), planes.rearrange("p t x -> p x t"), COPY)
+
+        def store_rows(b):
+            y = keep.tile([P, LANES, P], F32, name="y%d" % (b * P))
+            nc.scalar.copy(y[:], rows[b][:])
+            nc.scalar.dma_start(y_rows[:, :, b * P : (b + 1) * P], y[:])
+
+        y_third = summed_on_vector(2 * P, "first2")
+        y_grouped = keep.tile([P, V * LANES], BF16, name="y_grouped", tag="whole1", align_bytes=64)
+        round_on_scalar(y_grouped[:, : P * LANES], rows[0][:])
+        round_on_scalar(y_grouped[:, 2 * P * LANES : 3 * P * LANES], y_third[:])
+        store_rows(0)
+        round_on_scalar(y_grouped[:, P * LANES : 2 * P * LANES], rows[1][:])
+        store_rows(1)
+        y_last = summed_on_vector(3 * P, "first3")
+        nc.vector.tensor_copy(
+            y_grouped[:, 3 * P * LANES :].rearrange("p (c i t) -> p c t i", i=2, t=LANES),
+            y_last[:].rearrange("p t (c i) -> p c t i", i=2),
+        )
+        nc.vector.quantize_mx(out=y_codes[:].bitcast(E4), scales=y_scales[:], in_=y_grouped[:])
+        nc.sync.dma_start(y_words, y_codes[:])
         for q in range(4):
             queue = nc.sync if q % 2 == 0 else nc.scalar
             queue.dma_start(out_2[0, 4 * q : 4 * q + 4, :].bitcast(I32), y_scales[32 * q : 32 * q + 4, :].bitcast(I32))

@@ -12,10 +12,11 @@ BF16 = mybir.dt.bfloat16
 I32 = mybir.dt.int32
 U16 = mybir.dt.uint16
 U8 = mybir.dt.uint8
-E4 = mybir.dt.float8_e4m3fn_x4
-E5 = mybir.dt.float8_e5m2_x4
+E4M3 = mybir.dt.float8_e4m3fn_x4
+E5M2 = mybir.dt.float8_e5m2_x4
 MULT = mybir.AluOpType.mult
 ADD = mybir.AluOpType.add
+MAX = mybir.AluOpType.max
 RELU = mybir.ActivationFunctionType.Relu
 COPY = mybir.ActivationFunctionType.Copy
 
@@ -24,29 +25,35 @@ LANES = 4
 PASSES = DV // (P * LANES)
 HALF = 512
 HALVES = E // HALF
-CHUNK = 256
+STRIPE = 16
+QUADRANT = 32
+PART = HALF // 2
+DIRECT = PART
+TURNED = 2 * P
 SPARE = 32
-TURNED_NODES = 256
+RING = 8
 
 
 def tile_attend_gmp_pl_ew_kernel(tc, dyT, hE, ew, w_words, w_scales, offs, offs2, out_0, out_1, out_2):
     nc = tc.nc
     with ExitStack() as ctx:
         keep = ctx.enter_context(tc.tile_pool(name="keep", bufs=1))
-        ring = ctx.enter_context(tc.tile_pool(name="ring", bufs=8))
+        ring = ctx.enter_context(tc.tile_pool(name="ring", bufs=RING))
         psum = ctx.enter_context(tc.psum_pool(name="psum", bufs=1))
 
         dy_rows = dyT.rearrange("(o p t) v -> o t p v", p=P, t=LANES)
         h_rows = hE.rearrange("(o p t) e -> o p t e", p=P, t=LANES)
         units = [(half, o) for o in range(PASSES) for half in range(HALVES)]
+        u0, u1, u2, u3 = units
 
-        dst = keep.tile([P, E // 16], U16, name="dst")
-        src = keep.tile([P, E // 16], U16, name="src")
+        def h_tag(unit, t):
+            return "h%d%d%d" % (unit + (t,))
 
-        warm = keep.tile([P, 1], F32, name="warm")
-        warm2 = keep.tile([P, 1], F32, name="warm2")
-        nc.vector.memset(warm[:], 0.0)
-        nc.scalar.activation(warm2[:], warm[:], RELU, scale=2.0)
+        def product_tag(unit, e0):
+            return "product%d%d%d" % (unit + (e0,))
+
+        dst = keep.tile([P, E // STRIPE], U16, name="dst")
+        src = keep.tile([P, E // STRIPE], U16, name="src")
 
         ident = keep.tile([P, P], F32, name="ident")
         make_identity(nc, ident[:])
@@ -60,85 +67,89 @@ def tile_attend_gmp_pl_ew_kernel(tc, dyT, hE, ew, w_words, w_scales, offs, offs2
         nc.vector.memset(ws_raw[:].bitcast(I32), 0)
 
         h = {}
-        for half, o in units:
+        for unit in units:
             for t in range(LANES):
-                h[half, o, t] = keep.tile([P, HALF], F32, name="h%d%d%d" % (half, o, t), tag="h%d%d%d" % (half, o, t), align_bytes=64)
-        ew_sq = keep.tile([P, P], F32, name="ew_sq")
-        ew_row = keep.tile([P, CHUNK], F32, name="ew_row")
+                h[unit, t] = keep.tile([P, HALF], F32, name=h_tag(unit, t), tag=h_tag(unit, t), align_bytes=64)
+        ew_square = keep.tile([P, P], F32, name="ew_square")
+        ew_row = keep.tile([P, DIRECT], F32, name="ew_row")
         w_raw = keep.tile([P, PASSES, D], I32, name="w_raw", tag="w_raw", align_bytes=64)
 
         def load_h(unit, t, e0, e1):
             half, o = unit
-            nc.sync.dma_start(h[half, o, t][:, e0:e1], h_rows[o, :, t, half * HALF + e0 : half * HALF + e1])
+            nc.sync.dma_start(h[unit, t][:, e0:e1], h_rows[o, :, t, half * HALF + e0 : half * HALF + e1])
 
         for t in range(LANES):
-            load_h(units[0], t, 0, CHUNK)
+            load_h(u0, t, 0, PART)
             if t == 0:
                 nc.sync.dma_start(dst[:], offs)
             nc.sync.dma_start(dy[0, t][:, :V], dy_rows[0, t])
-        nc.sync.dma_start(ew_sq[:], ew[: P * P // E, :].rearrange("r (b e) -> (r b) e", e=P))
+        nc.sync.dma_start(ew_square[:], ew[: P * P // E, :].rearrange("r (b e) -> (r b) e", e=P))
         for t in range(LANES):
-            load_h(units[0], t, CHUNK, HALF)
-        for unit in units[1:3]:
+            load_h(u0, t, PART, HALF)
+        for unit in (u1, u2):
             for t in range(LANES):
                 load_h(unit, t, 0, HALF)
         for t in range(LANES):
             nc.sync.dma_start(dy[1, t][:, :V], dy_rows[1, t])
         for t in range(LANES):
-            load_h(units[3], t, 0, HALF)
-        for q in range(4):
+            load_h(u3, t, 0, HALF)
+        for q in range(P // QUADRANT):
             nc.sync.dma_start(
-                ws_raw[32 * q : 32 * q + 4, :, :].bitcast(I32),
+                ws_raw[QUADRANT * q : QUADRANT * q + 4, :, :].bitcast(I32),
                 w_scales[:, 4 * q : 4 * q + 4, :].rearrange("o f d -> f o d").bitcast(I32),
             )
         nc.sync.dma_start(w_raw[:], w_words.rearrange("o p d r -> p o (d r)").bitcast(I32))
-        nc.sync.dma_start(ew_row[:], ew[:, E - CHUNK :])
+        nc.sync.dma_start(ew_row[:], ew[:, E - DIRECT :])
         nc.sync.dma_start(src[:], offs2)
 
-        ew_ps = psum.tile([P, LANES, P], F32, name="ew_ps", tag="h")
-        nc.tensor.transpose(ew_ps[:, 0, :], ew_sq[:], ident[:])
+        ew_turned = psum.tile([P, LANES, P], F32, name="ew_turned", tag="h")
+        nc.tensor.transpose(ew_turned[:, 0, :], ew_square[:], ident[:])
         ew_col = keep.tile([P, E // P], F32, name="ew_col")
 
-        codes, scales, r, u = {}, {}, {}, {}
-        for half, o in units:
-            scales[half, o] = keep.tile([P, HALF], U8, name="scales%d%d" % (half, o), align_bytes=64)
+        codes, scales, slope, product = {}, {}, {}, {}
+        for unit in units:
+            scales[unit] = keep.tile([P, HALF], U8, name="scales%d%d" % unit, align_bytes=64)
 
         def relu(unit, e0, e1, lanes=range(LANES), tag=None):
-            if (unit, e0) not in r:
-                name = "r%d%d%d" % (unit + (e0,))
-                r[unit, e0] = keep.tile([P, LANES, e1 - e0], F32, name=name, tag=tag or name, align_bytes=64)
+            if (unit, e0) not in slope:
+                name = "slope%d%d%d" % (unit + (e0,))
+                slope[unit, e0] = keep.tile([P, LANES, e1 - e0], F32, name=name, tag=tag or name, align_bytes=64)
             for t in lanes:
-                nc.scalar.activation(r[unit, e0][:, t, :], h[unit + (t,)][:, e0:e1], RELU, scale=2.0)
+                if (unit, t) == (u2, LANES - 1):
+                    nc.vector.tensor_scalar(slope[unit, e0][:, t, :], h[unit, t][:, e0:e1], 2.0, 0.0, MULT, MAX)
+                else:
+                    nc.scalar.activation(slope[unit, e0][:, t, :], h[unit, t][:, e0:e1], RELU, scale=2.0)
 
-        def look_up(unit, e0, e1, tag=None):
+        def look_up(unit, e0, e1):
             half, o = unit
-            name = "u%d%d%d" % (half, o, e0)
-            u[unit, e0] = keep.tile([P, LANES, e1 - e0], F32, name=name, tag=tag or name, align_bytes=64)
-            picks = dst[:, (half * HALF + e0) // 16 : (half * HALF + e1) // 16]
+            name = product_tag(unit, e0)
+            product[unit, e0] = keep.tile([P, LANES, e1 - e0], F32, name=name, tag=name, align_bytes=64)
+            picks = dst[:, (half * HALF + e0) // STRIPE : (half * HALF + e1) // STRIPE]
             for t in range(LANES):
-                nc.vector.tensor_tensor(u[unit, e0][:, t, :], dy[o, t][:].indirect(picks), r[unit, e0][:, t, :], MULT)
+                nc.vector.tensor_tensor(
+                    product[unit, e0][:, t, :], dy[o, t][:].indirect(picks), slope[unit, e0][:, t, :], MULT
+                )
 
-        def quantise(unit, e0, n, grouped):
+        def quantise(unit, e0, edges, dz):
             if unit not in codes:
-                name = "codes%d%d" % unit
-                codes[unit] = keep.tile([P, HALF], I32, name=name, tag=name, align_bytes=64)
+                codes[unit] = keep.tile([P, HALF], I32, name="codes%d%d" % unit, align_bytes=64)
             nc.vector.quantize_mx(
-                out=codes[unit][:, e0 : e0 + n].bitcast(E5),
-                scales=scales[unit][:, e0 : e0 + n],
-                in_=grouped[:],
+                out=codes[unit][:, e0 : e0 + edges].bitcast(E5M2),
+                scales=scales[unit][:, e0 : e0 + edges],
+                in_=dz[:],
             )
 
-        back, grouped = {}, {}
+        back, staged = {}, {}
 
-        def weigh(unit, e0, b, bank, back_bank, spent=None):
-            half, o = unit
+        def weigh(unit, e0, b, bank, back_bank, tag=None):
+            half = unit[0]
             turned = psum.tile([P, LANES, P], F32, name="turned", tag=bank)
             for t in range(LANES):
-                nc.tensor.transpose(turned[:, t, :], u[unit, e0][:, t, b * P : (b + 1) * P], ident[:])
-            if spent:
-                pairs = keep.tile([P, 2 * P * 2], BF16, name="pairs", tag="h%d%d%d" % spent, align_bytes=64)
+                nc.tensor.transpose(turned[:, t, :], product[unit, e0][:, t, b * P : (b + 1) * P], ident[:])
+            if tag:
+                pairs = keep.tile([P, LANES * P], BF16, name="pairs", tag=tag, align_bytes=64)
             else:
-                pairs = ring.tile([P, 2 * P * 2], BF16, name="pairs")
+                pairs = ring.tile([P, LANES * P], BF16, name="pairs")
             block = (half * HALF + e0) // P + b
             nc.scalar.activation(
                 pairs[:].rearrange("e (w p s) -> e w p s", w=2, s=2),
@@ -150,28 +161,29 @@ def tile_attend_gmp_pl_ew_kernel(tc, dyT, hE, ew, w_words, w_scales, offs, offs2
             for w in range(2):
                 nc.tensor.transpose(back[unit, e0, b][:, w, :], pairs[:].bitcast(F32)[:, w * P : (w + 1) * P], ident[:])
 
-        def regroup(unit, e0, b, tag=None, group=2):
+        def regroup(unit, e0, b, tag=None):
+            blocks = 1 if tag else 2
             if tag:
-                grouped[unit] = keep.tile([P, group * P * LANES], BF16, name="grouped", tag=tag, align_bytes=64)
-            elif b % group == 0:
-                grouped[unit] = ring.tile([P, group * P * LANES], BF16, name="grouped", align_bytes=64)
-            at = (b % group) * 2 * P
+                staged[unit] = keep.tile([P, P * LANES], BF16, name="staged", tag=tag, align_bytes=64)
+            elif b % blocks == 0:
+                staged[unit] = ring.tile([P, blocks * P * LANES], BF16, name="staged", align_bytes=64)
+            at = (b % blocks) * 2 * P
             nc.scalar.copy(
-                grouped[unit][:].bitcast(F32)[:, at : at + 2 * P].rearrange("p (e w) -> p e w", w=2),
+                staged[unit][:].bitcast(F32)[:, at : at + 2 * P].rearrange("p (e w) -> p e w", w=2),
                 back[unit, e0, b][:].rearrange("p w e -> p e w"),
             )
-            if b % group == group - 1:
-                quantise(unit, e0 + (b + 1 - group) * P, group * P, grouped[unit])
+            if b % blocks == blocks - 1:
+                quantise(unit, e0 + (b + 1 - blocks) * P, blocks * P, staged[unit])
 
         def weigh_direct(unit, e0):
-            grouped = keep.tile([P, CHUNK * LANES], BF16, name="grouped_last", align_bytes=64)
+            dz = keep.tile([P, DIRECT * LANES], BF16, name="dz_direct", align_bytes=64)
             nc.vector.tensor_tensor(
-                grouped[:].rearrange("p (c i t) -> p c t i", i=2, t=LANES),
-                u[unit, e0][:].rearrange("p t (c i) -> p c t i", i=2),
-                ew_row[:].rearrange("p (c i) -> p c i", i=2).unsqueeze(2).to_broadcast([P, CHUNK // 2, LANES, 2]),
+                dz[:].rearrange("p (c i t) -> p c t i", i=2, t=LANES),
+                product[unit, e0][:].rearrange("p t (c i) -> p c t i", i=2),
+                ew_row[:].rearrange("p (c i) -> p c i", i=2).unsqueeze(2).to_broadcast([P, DIRECT // 2, LANES, 2]),
                 MULT,
             )
-            quantise(unit, e0, CHUNK, grouped)
+            quantise(unit, e0, DIRECT, dz)
 
         w_dealt, ws_dealt = {}, {}
 
@@ -190,109 +202,118 @@ def tile_attend_gmp_pl_ew_kernel(tc, dyT, hE, ew, w_words, w_scales, offs, offs2
 
         dm = {}
 
-        def multiply(half, t):
-            acc = psum.tile([P, HALF], F32, name="acc", tag=late[(2 * t + half) % len(late)])
+        def multiply(half, t, bank):
+            acc = psum.tile([P, HALF], F32, name="acc", tag=bank)
             for o in range(PASSES):
                 nc.tensor.matmul_mx(
                     out=acc[:],
-                    lhsT=w_dealt[t // 2][:, o, t % 2, :].bitcast(E4),
+                    lhsT=w_dealt[t // 2][:, o, t % 2, :].bitcast(E4M3),
                     lhsT_scale=ws_dealt[t // 2][:, o, t % 2, :],
-                    rhs=codes[half, o][:].bitcast(E5),
+                    rhs=codes[half, o][:].bitcast(E5M2),
                     rhs_scale=scales[half, o][:],
                     start=(o == 0),
                     stop=(o == PASSES - 1),
                 )
             if t not in dm:
-                dm[t] = keep.tile([P, E], F32, name="dm%d" % t, tag="dm%d" % t)
+                dm[t] = keep.tile([P, E], F32, name="dm%d" % t)
             nc.scalar.copy(dm[t][:, half * HALF : (half + 1) * HALF], acc[:])
 
-        u0, u1, u2, u3 = units
-        relu(u0, 0, CHUNK)
-        nc.scalar.copy(ew_col[:], ew_ps[:, 0, : E // P])
-        look_up(u0, 0, CHUNK)
-        relu(u0, CHUNK, HALF)
-        look_up(u0, CHUNK, HALF)
-        weigh(u0, 0, 0, "a", "a", u0 + (2,))
+        relu(u0, 0, PART)
+        nc.scalar.copy(ew_col[:], ew_turned[:, 0, : E // P])
+        look_up(u0, 0, PART)
+        relu(u0, PART, HALF)
+        look_up(u0, PART, HALF)
+        weigh(u0, 0, 0, "a", "a", h_tag(u0, 2))
         relu(u1, 0, HALF, range(1))
-        weigh(u0, 0, 1, "b", "c", u0 + (3,))
+        weigh(u0, 0, 1, "b", "c", h_tag(u0, 3))
         regroup(u0, 0, 0)
         regroup(u0, 0, 1)
+
         relu(u1, 0, HALF, range(1, LANES))
         look_up(u1, 0, HALF)
-        weigh(u0, CHUNK, 0, "b", "b", u1 + (2,))
-        weigh(u0, CHUNK, 1, "a", "c", u1 + (3,))
-        regroup(u0, CHUNK, 0)
-        regroup(u0, CHUNK, 1)
+        weigh(u0, PART, 0, "b", "b", h_tag(u1, 2))
+        weigh(u0, PART, 1, "a", "c", h_tag(u1, 3))
+        regroup(u0, PART, 0)
+        regroup(u0, PART, 1)
+
         relu(u2, 0, HALF)
         look_up(u2, 0, HALF)
-        weigh(u1, 0, 0, "a", "a", u2 + (2,))
-        weigh(u1, 0, 1, "b", "b", u2 + (3,))
+        weigh(u1, 0, 0, "a", "a", h_tag(u2, 2))
+        weigh(u1, 0, 1, "b", "b", h_tag(u2, 3))
         weigh(u1, 0, 2, "c", "c")
         regroup(u1, 0, 0)
-        relu(u3, 0, CHUNK, range(2))
+        relu(u3, 0, PART, range(2))
         weigh(u1, 0, 3, "a", "d")
-        relu(u3, 0, CHUNK, range(2, LANES))
-        for b in range(1, 4):
+        relu(u3, 0, PART, range(2, LANES))
+        for b in range(1, HALF // P):
             regroup(u1, 0, b)
-        look_up(u3, 0, CHUNK)
+
+        look_up(u3, 0, PART)
         weigh(u2, 0, 0, "a", "e")
         weigh(u2, 0, 1, "b", "f")
-        relu(u3, CHUNK, HALF, range(0, 1), "u100")
+        relu(u3, PART, HALF, range(0, 1), product_tag(u1, 0))
         weigh(u2, 0, 2, "c", "c")
-        relu(u3, CHUNK, HALF, range(1, 2))
+        relu(u3, PART, HALF, range(1, 2))
         weigh(u2, 0, 3, "d", "d")
-        relu(u3, CHUNK, HALF, range(2, 3))
+        relu(u3, PART, HALF, range(2, 3))
         regroup(u2, 0, 0)
-        relu(u3, CHUNK, HALF, range(3, 4))
-        look_up(u3, CHUNK, HALF)
+        relu(u3, PART, HALF, range(3, 4))
+        look_up(u3, PART, HALF)
         weigh(u3, 0, 0, "a", "a")
         regroup(u2, 0, 1)
         weigh(u3, 0, 1, "b", "g")
         regroup(u2, 0, 2)
         regroup(u2, 0, 3)
-        weigh_direct(u3, CHUNK)
-        deal(0, "h112", "h113")
-        regroup(u3, 0, 0, "next_to_last", 1)
-        regroup(u3, 0, 1, "last", 1)
+        weigh_direct(u3, PART)
+        deal(0, h_tag(u3, 2), h_tag(u3, 3))
+        regroup(u3, 0, 0, "next_to_last")
+        regroup(u3, 0, 1, "last")
         deal(1, "last", "w_raw")
-        late = ["b", "f", "b", "c", "a", "g", "d", "e"]
+
+        acc_banks = (("b", "f"), ("b", "c"), ("a", "g"), ("d", "e"))
         for t in range(LANES):
             for half in range(HALVES):
-                multiply(half, t)
+                multiply(half, t, acc_banks[t][half])
 
         y_rows = out_0.rearrange("(p t) x -> p t x", t=LANES)
         y_words = out_1[0].rearrange("p x r -> p (x r)").bitcast(I32)
         y_codes = keep.tile([P, V], I32, name="y_codes", align_bytes=64)
         y_scales = keep.tile([P, V], U8, name="y_scales", align_bytes=64)
 
-        first = [keep.tile([P, K * TURNED_NODES], F32, name="first%d" % t, tag="first%d" % t, align_bytes=64) for t in range(LANES)]
+        first = [
+            keep.tile([P, K * TURNED], F32, name="first%d" % t, tag="first%d" % t, align_bytes=64) for t in range(LANES)
+        ]
         for t in range(LANES):
-            nc.vector.tensor_copy(first[t][:], dm[t][:].indirect(src[:, : K * TURNED_NODES // 16]))
-        rows = {}
-        summed = [psum.tile([P, LANES, P], F32, name="summed", tag="bf"[b]) for b in range(TURNED_NODES // P)]
+            nc.vector.tensor_copy(first[t][:], dm[t][:].indirect(src[:, : K * TURNED // STRIPE]))
+        summed = [psum.tile([P, LANES, P], F32, name="summed", tag="bf"[b]) for b in range(TURNED // P)]
         for t in range(LANES):
-            for b in range(TURNED_NODES // P):
+            for b in range(TURNED // P):
                 for j in range(K):
                     nc.tensor.matmul(
-                        summed[b][:, t, :], first[t][:, b * K * P + j : (b + 1) * K * P : K], ident[:],
-                        start=(j == 0), stop=(j == K - 1), is_transpose=True,
+                        summed[b][:, t, :],
+                        first[t][:, b * K * P + j : (b + 1) * K * P : K],
+                        ident[:],
+                        start=(j == 0),
+                        stop=(j == K - 1),
+                        is_transpose=True,
                     )
-        for b in range(TURNED_NODES // P):
-            whole = keep.tile([P, LANES, P], F32, name="whole", tag="whole%d" % b, align_bytes=64)
-            nc.scalar.copy(whole[:], summed[b][:])
+        rows = {}
+        for b in range(TURNED // P):
+            sums = keep.tile([P, LANES, P], F32, name="sums", tag="sums%d" % b, align_bytes=64)
+            nc.scalar.copy(sums[:], summed[b][:])
             rows[b] = psum.tile([P, LANES, P], F32, name="rows", tag="ca"[b])
             for t in range(LANES):
-                nc.tensor.transpose(rows[b][:, t, :], whole[:, t, :], ident[:])
+                nc.tensor.transpose(rows[b][:, t, :], sums[:, t, :], ident[:])
 
-        def summed_on_vector(x0, tag):
+        def sum_on_vector(x0, tag):
             picked = keep.tile([P, LANES * K * P], F32, name="picked", tag=tag, align_bytes=64)
             y = keep.tile([P, LANES, P], F32, name="y%d" % x0)
             for t in range(LANES):
                 nc.vector.tensor_copy(
                     picked[:, t * K * P : (t + 1) * K * P],
-                    dm[t][:].indirect(src[:, K * x0 // 16 : K * (x0 + P) // 16]),
+                    dm[t][:].indirect(src[:, K * x0 // STRIPE : K * (x0 + P) // STRIPE]),
                 )
-            for pair in range(2):
+            for pair in range(LANES // 2):
                 nc.vector.tensor_tensor(
                     y[:, 2 * pair : 2 * pair + 2, :].rearrange("p s x -> p (s x)"),
                     picked[:, 2 * pair * K * P : 2 * (pair + 1) * K * P : K],
@@ -302,28 +323,34 @@ def tile_attend_gmp_pl_ew_kernel(tc, dyT, hE, ew, w_words, w_scales, offs, offs2
             nc.sync.dma_start(y_rows[:, :, x0 : x0 + P], y[:])
             return y
 
-        def round_on_scalar(grouped, planes):
-            nc.scalar.activation(grouped.rearrange("p (x t) -> p x t", t=LANES), planes.rearrange("p t x -> p x t"), COPY)
+        def round_on_scalar(b, lanes):
+            nc.scalar.activation(
+                y_bf16[:, b * P * LANES : (b + 1) * P * LANES].rearrange("p (x t) -> p x t", t=LANES),
+                lanes.rearrange("p t x -> p x t"),
+                COPY,
+            )
 
         def store_rows(b):
             y = keep.tile([P, LANES, P], F32, name="y%d" % (b * P))
             nc.scalar.copy(y[:], rows[b][:])
             nc.scalar.dma_start(y_rows[:, :, b * P : (b + 1) * P], y[:])
 
-        y_third = summed_on_vector(2 * P, "first2")
-        y_grouped = keep.tile([P, V * LANES], BF16, name="y_grouped", tag="whole1", align_bytes=64)
-        round_on_scalar(y_grouped[:, : P * LANES], rows[0][:])
-        round_on_scalar(y_grouped[:, 2 * P * LANES : 3 * P * LANES], y_third[:])
+        y_third = sum_on_vector(2 * P, "first2")
+        y_bf16 = keep.tile([P, V * LANES], BF16, name="y_bf16", tag="sums1", align_bytes=64)
+        round_on_scalar(0, rows[0][:])
+        round_on_scalar(2, y_third[:])
         store_rows(0)
-        round_on_scalar(y_grouped[:, P * LANES : 2 * P * LANES], rows[1][:])
         store_rows(1)
-        y_last = summed_on_vector(3 * P, "first3")
+        round_on_scalar(1, rows[1][:])
+        y_last = sum_on_vector(3 * P, "first3")
         nc.vector.tensor_copy(
-            y_grouped[:, 3 * P * LANES :].rearrange("p (c i t) -> p c t i", i=2, t=LANES),
+            y_bf16[:, 3 * P * LANES :].rearrange("p (c i t) -> p c t i", i=2, t=LANES),
             y_last[:].rearrange("p t (c i) -> p c t i", i=2),
         )
-        nc.vector.quantize_mx(out=y_codes[:].bitcast(E4), scales=y_scales[:], in_=y_grouped[:])
+        nc.vector.quantize_mx(out=y_codes[:].bitcast(E4M3), scales=y_scales[:], in_=y_bf16[:])
         nc.sync.dma_start(y_words, y_codes[:])
-        for q in range(4):
+        for q in range(P // QUADRANT):
             queue = nc.sync if q % 2 == 0 else nc.scalar
-            queue.dma_start(out_2[0, 4 * q : 4 * q + 4, :].bitcast(I32), y_scales[32 * q : 32 * q + 4, :].bitcast(I32))
+            queue.dma_start(
+                out_2[0, 4 * q : 4 * q + 4, :].bitcast(I32), y_scales[QUADRANT * q : QUADRANT * q + 4, :].bitcast(I32)
+            )

from contextlib import ExitStack

import concourse.mybir as mybir
from concourse.masks import make_identity

V, K, E, D, DV = 512, 2, 1024, 512, 1024
FLOPS = 2 * DV * D * E
BYTES = 4 * DV * V + 4 * DV * E + 4 * E + DV * D + DV * D // 32 + 2 * 2 * 128 * 64 + 4 * D * V + D * V + D * V // 32

F32 = mybir.dt.float32
BF16 = mybir.dt.bfloat16
I32 = mybir.dt.int32
U16 = mybir.dt.uint16
U8 = mybir.dt.uint8
E4M3 = mybir.dt.float8_e4m3fn_x4
E5M2 = mybir.dt.float8_e5m2_x4
MULT = mybir.AluOpType.mult
ADD = mybir.AluOpType.add
MAX = mybir.AluOpType.max
RELU = mybir.ActivationFunctionType.Relu
COPY = mybir.ActivationFunctionType.Copy

P = 128
LANES = 4
PASSES = DV // (P * LANES)
HALF = 512
HALVES = E // HALF
STRIPE = 16
QUADRANT = 32
PART = HALF // 2
DIRECT = PART
TURNED = 2 * P
SPARE = 32
RING = 8


def tile_attend_gmp_pl_ew_kernel(tc, dyT, hE, ew, w_words, w_scales, offs, offs2, out_0, out_1, out_2):
    nc = tc.nc
    with ExitStack() as ctx:
        keep = ctx.enter_context(tc.tile_pool(name="keep", bufs=1))
        ring = ctx.enter_context(tc.tile_pool(name="ring", bufs=RING))
        psum = ctx.enter_context(tc.psum_pool(name="psum", bufs=1))

        dy_rows = dyT.rearrange("(o p t) v -> o t p v", p=P, t=LANES)
        h_rows = hE.rearrange("(o p t) e -> o p t e", p=P, t=LANES)
        units = [(half, o) for o in range(PASSES) for half in range(HALVES)]
        u0, u1, u2, u3 = units

        def h_tag(unit, t):
            return "h%d%d%d" % (unit + (t,))

        def product_tag(unit, e0):
            return "product%d%d%d" % (unit + (e0,))

        dst = keep.tile([P, E // STRIPE], U16, name="dst")
        src = keep.tile([P, E // STRIPE], U16, name="src")

        ident = keep.tile([P, P], F32, name="ident")
        make_identity(nc, ident[:])

        dy = {}
        for o in range(PASSES):
            for t in range(LANES):
                dy[o, t] = keep.tile([P, V + SPARE], F32, name="dy%d%d" % (o, t))
                nc.vector.memset(dy[o, t][:, V:], 0.0)
        ws_raw = keep.tile([P, PASSES, D], U8, name="ws_raw")
        nc.vector.memset(ws_raw[:].bitcast(I32), 0)

        h = {}
        for unit in units:
            for t in range(LANES):
                h[unit, t] = keep.tile([P, HALF], F32, name=h_tag(unit, t), tag=h_tag(unit, t), align_bytes=64)
        ew_square = keep.tile([P, P], F32, name="ew_square")
        ew_row = keep.tile([P, DIRECT], F32, name="ew_row")
        w_raw = keep.tile([P, PASSES, D], I32, name="w_raw", tag="w_raw", align_bytes=64)

        def load_h(unit, t, e0, e1):
            half, o = unit
            nc.sync.dma_start(h[unit, t][:, e0:e1], h_rows[o, :, t, half * HALF + e0 : half * HALF + e1])

        for t in range(LANES):
            load_h(u0, t, 0, PART)
            if t == 0:
                nc.sync.dma_start(dst[:], offs)
            nc.sync.dma_start(dy[0, t][:, :V], dy_rows[0, t])
        nc.sync.dma_start(ew_square[:], ew[: P * P // E, :].rearrange("r (b e) -> (r b) e", e=P))
        for t in range(LANES):
            load_h(u0, t, PART, HALF)
        for unit in (u1, u2):
            for t in range(LANES):
                load_h(unit, t, 0, HALF)
        for t in range(LANES):
            nc.sync.dma_start(dy[1, t][:, :V], dy_rows[1, t])
        for t in range(LANES):
            load_h(u3, t, 0, HALF)
        for q in range(P // QUADRANT):
            nc.sync.dma_start(
                ws_raw[QUADRANT * q : QUADRANT * q + 4, :, :].bitcast(I32),
                w_scales[:, 4 * q : 4 * q + 4, :].rearrange("o f d -> f o d").bitcast(I32),
            )
        nc.sync.dma_start(w_raw[:], w_words.rearrange("o p d r -> p o (d r)").bitcast(I32))
        nc.sync.dma_start(ew_row[:], ew[:, E - DIRECT :])
        nc.sync.dma_start(src[:], offs2)

        ew_turned = psum.tile([P, LANES, P], F32, name="ew_turned", tag="h")
        nc.tensor.transpose(ew_turned[:, 0, :], ew_square[:], ident[:])
        ew_col = keep.tile([P, E // P], F32, name="ew_col")

        codes, scales, slope, product = {}, {}, {}, {}
        for unit in units:
            scales[unit] = keep.tile([P, HALF], U8, name="scales%d%d" % unit, align_bytes=64)

        def relu(unit, e0, e1, lanes=range(LANES), tag=None):
            if (unit, e0) not in slope:
                name = "slope%d%d%d" % (unit + (e0,))
                slope[unit, e0] = keep.tile([P, LANES, e1 - e0], F32, name=name, tag=tag or name, align_bytes=64)
            for t in lanes:
                if (unit, t) == (u2, LANES - 1):
                    nc.vector.tensor_scalar(slope[unit, e0][:, t, :], h[unit, t][:, e0:e1], 2.0, 0.0, MULT, MAX)
                else:
                    nc.scalar.activation(slope[unit, e0][:, t, :], h[unit, t][:, e0:e1], RELU, scale=2.0)

        def look_up(unit, e0, e1):
            half, o = unit
            name = product_tag(unit, e0)
            product[unit, e0] = keep.tile([P, LANES, e1 - e0], F32, name=name, tag=name, align_bytes=64)
            picks = dst[:, (half * HALF + e0) // STRIPE : (half * HALF + e1) // STRIPE]
            for t in range(LANES):
                nc.vector.tensor_tensor(
                    product[unit, e0][:, t, :], dy[o, t][:].indirect(picks), slope[unit, e0][:, t, :], MULT
                )

        def quantise(unit, e0, edges, dz):
            if unit not in codes:
                codes[unit] = keep.tile([P, HALF], I32, name="codes%d%d" % unit, align_bytes=64)
            nc.vector.quantize_mx(
                out=codes[unit][:, e0 : e0 + edges].bitcast(E5M2),
                scales=scales[unit][:, e0 : e0 + edges],
                in_=dz[:],
            )

        back, staged = {}, {}

        def weigh(unit, e0, b, bank, back_bank, tag=None):
            half = unit[0]
            turned = psum.tile([P, LANES, P], F32, name="turned", tag=bank)
            for t in range(LANES):
                nc.tensor.transpose(turned[:, t, :], product[unit, e0][:, t, b * P : (b + 1) * P], ident[:])
            if tag:
                pairs = keep.tile([P, LANES * P], BF16, name="pairs", tag=tag, align_bytes=64)
            else:
                pairs = ring.tile([P, LANES * P], BF16, name="pairs")
            block = (half * HALF + e0) // P + b
            nc.scalar.activation(
                pairs[:].rearrange("e (w p s) -> e w p s", w=2, s=2),
                turned[:].rearrange("e (w s) p -> e w p s", s=2),
                COPY,
                scale=ew_col[:, block : block + 1],
            )
            back[unit, e0, b] = psum.tile([P, 2, P], F32, name="back", tag=back_bank)
            for w in range(2):
                nc.tensor.transpose(back[unit, e0, b][:, w, :], pairs[:].bitcast(F32)[:, w * P : (w + 1) * P], ident[:])

        def regroup(unit, e0, b, tag=None):
            blocks = 1 if tag else 2
            if tag:
                staged[unit] = keep.tile([P, P * LANES], BF16, name="staged", tag=tag, align_bytes=64)
            elif b % blocks == 0:
                staged[unit] = ring.tile([P, blocks * P * LANES], BF16, name="staged", align_bytes=64)
            at = (b % blocks) * 2 * P
            nc.scalar.copy(
                staged[unit][:].bitcast(F32)[:, at : at + 2 * P].rearrange("p (e w) -> p e w", w=2),
                back[unit, e0, b][:].rearrange("p w e -> p e w"),
            )
            if b % blocks == blocks - 1:
                quantise(unit, e0 + (b + 1 - blocks) * P, blocks * P, staged[unit])

        def weigh_direct(unit, e0):
            dz = keep.tile([P, DIRECT * LANES], BF16, name="dz_direct", align_bytes=64)
            nc.vector.tensor_tensor(
                dz[:].rearrange("p (c i t) -> p c t i", i=2, t=LANES),
                product[unit, e0][:].rearrange("p t (c i) -> p c t i", i=2),
                ew_row[:].rearrange("p (c i) -> p c i", i=2).unsqueeze(2).to_broadcast([P, DIRECT // 2, LANES, 2]),
                MULT,
            )
            quantise(unit, e0, DIRECT, dz)

        w_dealt, ws_dealt = {}, {}

        def deal(pair, words_tag, scales_tag):
            w_dealt[pair] = keep.tile([P, PASSES, 2, P], I32, name="w_dealt%d" % pair, tag=words_tag, align_bytes=64)
            ws_dealt[pair] = keep.tile([P, PASSES, 2, P], U8, name="ws_dealt%d" % pair, tag=scales_tag, align_bytes=64)
            lanes = slice(2 * pair, 2 * pair + 2)
            nc.vector.tensor_copy(
                w_dealt[pair][:].rearrange("p o s (c i) -> p o c s i", i=4),
                w_raw[:].rearrange("p o (c i t) -> p o c t i", t=LANES, i=4)[:, :, :, lanes, :],
            )
            nc.vector.tensor_copy(
                ws_dealt[pair][:],
                ws_raw[:].rearrange("p o (m t) -> p o t m", t=LANES)[:, :, lanes, :],
            )

        dm = {}

        def multiply(half, t, bank):
            acc = psum.tile([P, HALF], F32, name="acc", tag=bank)
            for o in range(PASSES):
                nc.tensor.matmul_mx(
                    out=acc[:],
                    lhsT=w_dealt[t // 2][:, o, t % 2, :].bitcast(E4M3),
                    lhsT_scale=ws_dealt[t // 2][:, o, t % 2, :],
                    rhs=codes[half, o][:].bitcast(E5M2),
                    rhs_scale=scales[half, o][:],
                    start=(o == 0),
                    stop=(o == PASSES - 1),
                )
            if t not in dm:
                dm[t] = keep.tile([P, E], F32, name="dm%d" % t)
            nc.scalar.copy(dm[t][:, half * HALF : (half + 1) * HALF], acc[:])

        relu(u0, 0, PART)
        nc.scalar.copy(ew_col[:], ew_turned[:, 0, : E // P])
        look_up(u0, 0, PART)
        relu(u0, PART, HALF)
        look_up(u0, PART, HALF)
        weigh(u0, 0, 0, "a", "a", h_tag(u0, 2))
        relu(u1, 0, HALF, range(1))
        weigh(u0, 0, 1, "b", "c", h_tag(u0, 3))
        regroup(u0, 0, 0)
        regroup(u0, 0, 1)

        relu(u1, 0, HALF, range(1, LANES))
        look_up(u1, 0, HALF)
        weigh(u0, PART, 0, "b", "b", h_tag(u1, 2))
        weigh(u0, PART, 1, "a", "c", h_tag(u1, 3))
        regroup(u0, PART, 0)
        regroup(u0, PART, 1)

        relu(u2, 0, HALF)
        look_up(u2, 0, HALF)
        weigh(u1, 0, 0, "a", "a", h_tag(u2, 2))
        weigh(u1, 0, 1, "b", "b", h_tag(u2, 3))
        weigh(u1, 0, 2, "c", "c")
        regroup(u1, 0, 0)
        relu(u3, 0, PART, range(2))
        weigh(u1, 0, 3, "a", "d")
        relu(u3, 0, PART, range(2, LANES))
        for b in range(1, HALF // P):
            regroup(u1, 0, b)

        look_up(u3, 0, PART)
        weigh(u2, 0, 0, "a", "e")
        weigh(u2, 0, 1, "b", "f")
        relu(u3, PART, HALF, range(0, 1), product_tag(u1, 0))
        weigh(u2, 0, 2, "c", "c")
        relu(u3, PART, HALF, range(1, 2))
        weigh(u2, 0, 3, "d", "d")
        relu(u3, PART, HALF, range(2, 3))
        regroup(u2, 0, 0)
        relu(u3, PART, HALF, range(3, 4))
        look_up(u3, PART, HALF)
        weigh(u3, 0, 0, "a", "a")
        regroup(u2, 0, 1)
        weigh(u3, 0, 1, "b", "g")
        regroup(u2, 0, 2)
        regroup(u2, 0, 3)
        weigh_direct(u3, PART)
        deal(0, h_tag(u3, 2), h_tag(u3, 3))
        regroup(u3, 0, 0, "next_to_last")
        regroup(u3, 0, 1, "last")
        deal(1, "last", "w_raw")

        acc_banks = (("b", "f"), ("b", "c"), ("a", "g"), ("d", "e"))
        for t in range(LANES):
            for half in range(HALVES):
                multiply(half, t, acc_banks[t][half])

        y_rows = out_0.rearrange("(p t) x -> p t x", t=LANES)
        y_words = out_1[0].rearrange("p x r -> p (x r)").bitcast(I32)
        y_codes = keep.tile([P, V], I32, name="y_codes", align_bytes=64)
        y_scales = keep.tile([P, V], U8, name="y_scales", align_bytes=64)

        first = [
            keep.tile([P, K * TURNED], F32, name="first%d" % t, tag="first%d" % t, align_bytes=64) for t in range(LANES)
        ]
        for t in range(LANES):
            nc.vector.tensor_copy(first[t][:], dm[t][:].indirect(src[:, : K * TURNED // STRIPE]))
        summed = [psum.tile([P, LANES, P], F32, name="summed", tag="bf"[b]) for b in range(TURNED // P)]
        for t in range(LANES):
            for b in range(TURNED // P):
                for j in range(K):
                    nc.tensor.matmul(
                        summed[b][:, t, :],
                        first[t][:, b * K * P + j : (b + 1) * K * P : K],
                        ident[:],
                        start=(j == 0),
                        stop=(j == K - 1),
                        is_transpose=True,
                    )
        rows = {}
        for b in range(TURNED // P):
            sums = keep.tile([P, LANES, P], F32, name="sums", tag="sums%d" % b, align_bytes=64)
            nc.scalar.copy(sums[:], summed[b][:])
            rows[b] = psum.tile([P, LANES, P], F32, name="rows", tag="ca"[b])
            for t in range(LANES):
                nc.tensor.transpose(rows[b][:, t, :], sums[:, t, :], ident[:])

        def sum_on_vector(x0, tag):
            picked = keep.tile([P, LANES * K * P], F32, name="picked", tag=tag, align_bytes=64)
            y = keep.tile([P, LANES, P], F32, name="y%d" % x0)
            for t in range(LANES):
                nc.vector.tensor_copy(
                    picked[:, t * K * P : (t + 1) * K * P],
                    dm[t][:].indirect(src[:, K * x0 // STRIPE : K * (x0 + P) // STRIPE]),
                )
            for pair in range(LANES // 2):
                nc.vector.tensor_tensor(
                    y[:, 2 * pair : 2 * pair + 2, :].rearrange("p s x -> p (s x)"),
                    picked[:, 2 * pair * K * P : 2 * (pair + 1) * K * P : K],
                    picked[:, 2 * pair * K * P + 1 : 2 * (pair + 1) * K * P : K],
                    ADD,
                )
            nc.sync.dma_start(y_rows[:, :, x0 : x0 + P], y[:])
            return y

        def round_on_scalar(b, lanes):
            nc.scalar.activation(
                y_bf16[:, b * P * LANES : (b + 1) * P * LANES].rearrange("p (x t) -> p x t", t=LANES),
                lanes.rearrange("p t x -> p x t"),
                COPY,
            )

        def store_rows(b):
            y = keep.tile([P, LANES, P], F32, name="y%d" % (b * P))
            nc.scalar.copy(y[:], rows[b][:])
            nc.scalar.dma_start(y_rows[:, :, b * P : (b + 1) * P], y[:])

        y_third = sum_on_vector(2 * P, "first2")
        y_bf16 = keep.tile([P, V * LANES], BF16, name="y_bf16", tag="sums1", align_bytes=64)
        round_on_scalar(0, rows[0][:])
        round_on_scalar(2, y_third[:])
        store_rows(0)
        store_rows(1)
        round_on_scalar(1, rows[1][:])
        y_last = sum_on_vector(3 * P, "first3")
        nc.vector.tensor_copy(
            y_bf16[:, 3 * P * LANES :].rearrange("p (c i t) -> p c t i", i=2, t=LANES),
            y_last[:].rearrange("p t (c i) -> p c t i", i=2),
        )
        nc.vector.quantize_mx(out=y_codes[:].bitcast(E4M3), scales=y_scales[:], in_=y_bf16[:])
        nc.sync.dma_start(y_words, y_codes[:])
        for q in range(P // QUADRANT):
            queue = nc.sync if q % 2 == 0 else nc.scalar
            queue.dma_start(
                out_2[0, 4 * q : 4 * q + 4, :].bitcast(I32), y_scales[QUADRANT * q : QUADRANT * q + 4, :].bitcast(I32)
            )
